import numpy as np
import ml_dtypes


def mxq(x, axis, fmt="e4m3"):
    dtype, down = {"e4m3": (ml_dtypes.float8_e4m3fn, 7), "e5m2": (ml_dtypes.float8_e5m2, 14)}[fmt]
    v = np.moveaxis(np.asarray(x, np.float32).astype(ml_dtypes.bfloat16).astype(np.float64), axis, -1)
    blocks = v.reshape(v.shape[:-1] + (-1, 32))
    amax = np.abs(blocks).max(-1, keepdims=True)
    byte = np.maximum(np.where(amax > 0, np.frexp(amax)[1] - 1 + 127, 0) - down, 1)
    scale = np.exp2(byte - 127.0)
    codes = (blocks / scale).astype(np.float32).astype(dtype).astype(np.float64)
    return np.moveaxis((codes * scale).reshape(v.shape), -1, axis)


WIDE = False


def mx_kscale(k):
    if not WIDE:
        return np.ones(k)
    levels = np.array([10, -10, 5, -5, 0])
    if k % 512:
        return np.exp2(np.random.permutation(np.resize(levels, k // 32))).repeat(32)
    a = np.empty((k // 512, 16))
    for p in range(k // 512):
        a[p, :8] = np.random.permutation(np.resize(levels, 8))
        for g in range(8):
            far = levels[np.abs(levels - a[p, g]) >= 10]
            a[p, g + 8] = far[np.random.randint(len(far))]
    return np.exp2(a.ravel()).repeat(32)


def f64(x):
    return np.asarray(x).astype(np.float64)


def striped(idx):
    return np.tile(np.asarray(idx).reshape(-1, 16).T, (8, 1)).astype(np.uint16)


def unstriped(offs):
    return offs[:16].T.reshape(-1).astype(np.int64)


E2M1 = np.array([0.0, 0.5, 1.0, 1.5, 2.0, 3.0, 4.0, 6.0, -0.0, -0.5, -1.0, -1.5, -2.0, -3.0, -4.0, -6.0])


def pack_weight(w, fmt):
    k, n = w.shape
    w = f64(np.asarray(w, np.float32).astype(ml_dtypes.bfloat16)).reshape(k // 32, 32, n)
    amax = np.abs(w).max(1)
    if fmt == "e4m3":
        byte = np.frexp(amax)[1] - 1 + 127 - 7
    else:
        mant, ex = np.frexp(amax / 6.0)
        byte = np.where(mant > 0.5, ex, ex - 1) + 127
    byte = np.clip(np.where(amax > 0, byte, 1), 1, 254)
    scaled = (w * np.exp2(127.0 - byte)[:, None, :]).reshape(k, n).astype(np.float32)
    by_word = np.ascontiguousarray(scaled.reshape(k // 512, 128, 4, n).transpose(0, 1, 3, 2))
    if fmt == "e4m3":
        words = by_word.astype(ml_dtypes.float8_e4m3fn).view(np.uint8)
    else:
        c = by_word.astype(ml_dtypes.float4_e2m1fn).view(np.uint8) & 0xF
        words = (c[..., 0::2] | (c[..., 1::2] << 4)).reshape(k // 512, 128, 2 * n)
    return np.ascontiguousarray(words), np.ascontiguousarray(byte.astype(np.uint8).reshape(k // 512, 16, n))


def unpack_weight(words, scales, fmt):
    g, _, n = scales.shape
    words = np.ascontiguousarray(words).reshape(g, 128, n, -1)
    if fmt == "e4m3":
        vals = words.view(ml_dtypes.float8_e4m3fn).astype(np.float64)
    else:
        nib = np.empty((g, 128, n, 4), np.uint8)
        nib[..., 0::2] = words & 0xF
        nib[..., 1::2] = words >> 4
        vals = E2M1[nib]
    vals = vals * np.repeat(np.exp2(scales.astype(np.float64) - 127.0), 8, axis=1)[..., None]
    return vals.transpose(0, 1, 3, 2).reshape(g * 512, n)


def bf(x):
    return np.asarray(x, np.float32).astype(ml_dtypes.bfloat16)


def planes(Y):
    r, m = Y.shape
    b = f64(bf(Y)).reshape(r // 32, 32, m)
    amax = np.abs(b).max(1)
    byte = np.clip(np.where(amax > 0, np.frexp(amax)[1] - 1 + 127 - 7, 1), 1, 254)
    codes = (b * np.exp2(127.0 - byte)[:, None, :]).reshape(r, m).astype(np.float32).astype(ml_dtypes.float8_e4m3fn).view(np.uint8)
    words = codes.reshape(r // 512, 128, 4, m).transpose(0, 1, 3, 2)
    return np.ascontiguousarray(words), np.ascontiguousarray(byte.astype(np.uint8).reshape(r // 512, 16, m))


K, T, J, I, N = 512, 2048, 1024, 512, 512


def setup_inputs():
    n = np.random.standard_normal
    idx = np.random.permutation(T)[:J]
    idx2 = np.random.permutation(J)[:I]
    fk = mx_kscale(K)
    wap = pack_weight(n((K, N)) * 1 / np.sqrt(K) * fk[:, None], "e4m3")
    wbp = pack_weight(n((K, N)) * 1 / np.sqrt(K) * fk[:, None], "e2m1")
    return {
        "xf": (n((K, T)) / fk[:, None]).astype(np.float32),
        "wa_words": wap[0],
        "wa_scales": wap[1],
        "wb_words": wbp[0],
        "wb_scales": wbp[1],
        "offs": striped(idx),
        "offs2": striped(idx2),
    }


def reference(xf, wa_words, wa_scales, wb_words, wb_scales, offs, offs2):
    idx = unstriped(offs)
    idx2 = unstriped(offs2)
    wau = unpack_weight(wa_words, wa_scales, "e4m3")
    wbu = unpack_weight(wb_words, wb_scales, "e2m1")
    xg = f64(xf)[:, idx]
    xgq = mxq(xg, 0, "e4m3")
    p = wau.T @ xgq
    xgidx2q = mxq(xg[:, idx2], 0, "e4m3")
    q = wbu.T @ xgidx2q
    qs = np.zeros((N, J))
    qs[:, idx2] = q
    y = p + qs
    words, scales = planes(y)
    return y, words, scales

@@ -1,0 +1,226 @@
+from contextlib import ExitStack
+
+import concourse.mybir as mybir
+
+K, T, J, I, N = 512, 2048, 1024, 512, 512
+FLOPS = 2 * K * N * (J + I)
+
+F32 = mybir.dt.float32
+BF16 = mybir.dt.bfloat16
+I32 = mybir.dt.int32
+U32 = mybir.dt.uint32
+U16 = mybir.dt.uint16
+U8 = mybir.dt.uint8
+FP8X4 = mybir.dt.float8_e4m3fn_x4
+FP4X4 = mybir.dt.float4_e2m1fn_x4
+ADD = mybir.AluOpType.add
+
+P = 128
+PACK = 4
+BANK = 512
+HALF = I // 2
+CHUNK = 256
+
+
+def weave(engine_copy, woven, planes, pair, cols):
+    engine_copy(
+        out=woven[:, cols, 2 * pair : 2 * pair + 2],
+        in_=planes[:, :, cols].rearrange("p t c -> p c t"),
+    )
+
+
+def quantize(nc, codes, scales, woven, cols):
+    nc.vector.quantize_mx(
+        out=codes[:, cols].bitcast(FP8X4),
+        scales=scales[:, cols],
+        in_=woven[:, cols, :].rearrange("p c t -> p (c t)"),
+    )
+
+
+def tile_list_two_level_routing_pl_kernel(tc, xf, wa_words, wa_scales, wb_words, wb_scales, offs, offs2, out_0, out_1, out_2):
+    nc = tc.nc
+    with ExitStack() as ctx:
+        lists = ctx.enter_context(tc.tile_pool(name="lists", bufs=1))
+        keep = ctx.enter_context(tc.tile_pool(name="keep", bufs=1))
+        psum = ctx.enter_context(tc.psum_pool(name="psum", bufs=1))
+
+        offs_sb = lists.tile([P, J // 16], U16, name="offs_sb")
+        offs2_sb = lists.tile([P, I // 16], U16, name="offs2_sb")
+
+        x_rows = xf.rearrange("(p t) c -> t p c", t=PACK)
+        x_planes = [keep.tile([P, T], F32, name="x_plane%d" % t, tag="x_plane%d" % t) for t in range(PACK)]
+        wa_raw = keep.tile([P, N], U32, name="wa_raw", align_bytes=64)
+        wb_raw = keep.tile([P, 2 * N], U8, name="wb_raw", align_bytes=64)
+        sc_raw = keep.tile([P, 2 * N], U8, name="sc_raw", align_bytes=64)
+        wa = keep.tile([P, N], U32, name="wa", align_bytes=64)
+        wb = keep.tile([P, 2 * N], U8, name="wb", align_bytes=64)
+        sc = keep.tile([P, 2 * N], U8, name="sc", align_bytes=64)
+        pages = [keep.tile([P, J], F32, name="page%d" % t) for t in range(PACK)]
+
+        nc.vector.memset(sc_raw[:].bitcast(I32), 0)
+        nc.sync.dma_start(offs_sb[:], offs)
+        nc.sync.dma_start(out=wb_raw[:].bitcast(I32), in_=wb_words[0].bitcast(I32))
+        nc.sync.dma_start(out=x_planes[0][:], in_=x_rows[0])
+        for w, w_scales in enumerate((wa_scales, wb_scales)):
+            for q in range(4):
+                nc.scalar.dma_start(
+                    out=sc_raw[32 * q : 32 * q + 4, w * N : (w + 1) * N].bitcast(I32),
+                    in_=w_scales[0, 4 * q : 4 * q + 4, :].bitcast(I32),
+                )
+        nc.sync.dma_start(offs2_sb[:], offs2)
+        for t in range(1, PACK):
+            nc.sync.dma_start(out=x_planes[t][:], in_=x_rows[t])
+        nc.sync.dma_start(out=wa_raw[:].bitcast(I32), in_=wa_words[0].rearrange("p n t -> p (n t)").bitcast(I32))
+
+        for t in range(PACK):
+            nc.vector.memset(pages[t][:].bitcast(I32), 0)
+        nc.vector.tensor_copy(
+            out=wb[:].bitcast(U16).rearrange("p (t m) -> p t m", t=PACK),
+            in_=wb_raw[:].bitcast(U16).rearrange("p (m t) -> p t m", t=PACK),
+        )
+        nc.vector.tensor_copy(
+            out=sc[:].rearrange("p (w t m) -> p w t m", w=2, t=PACK),
+            in_=sc_raw[:].rearrange("p (w m t) -> p w t m", w=2, t=PACK),
+        )
+
+        xg = keep.tile([P, PACK, J], F32, name="xg")
+        xe0 = keep.tile([P, PACK, HALF], F32, name="xe0")
+        xe0_woven = keep.tile([P, HALF, PACK], BF16, name="xe0_woven", tag="hold_a", align_bytes=64)
+        xe0_codes = keep.tile([P, HALF], U32, name="xe0_codes", tag="hold_b", align_bytes=64)
+        xe0_scales = keep.tile([P, HALF], U8, name="xe0_scales", tag="hold_c", align_bytes=64)
+        xe1_codes = keep.tile([P, HALF], U32, name="xe1_codes", align_bytes=64)
+        xe1_scales = keep.tile([P, HALF], U8, name="xe1_scales", align_bytes=64)
+        xg_codes = keep.tile([P, J], U32, name="xg_codes", align_bytes=64)
+        xg_scales = keep.tile([P, J], U8, name="xg_scales", align_bytes=64)
+        half_offs = [offs2_sb[:, h * (HALF // 16) : (h + 1) * (HALF // 16)] for h in range(2)]
+        whole = slice(0, HALF)
+        banks = [slice(b * BANK, (b + 1) * BANK) for b in range(J // BANK)]
+        chunks = [slice(c, c + CHUNK) for c in range(0, J, CHUNK)]
+
+        def expert(acc, t, codes, scales):
+            nc.tensor.matmul_mx(
+                out=acc,
+                lhsT=wb[:, 2 * P * t : 2 * P * (t + 1)].bitcast(FP4X4),
+                lhsT_scale=sc[:, N + P * t : N + P * (t + 1)],
+                rhs=codes[:].bitcast(FP8X4),
+                rhs_scale=scales[:],
+                start=True,
+                stop=True,
+            )
+
+        def scatter(t, h, values):
+            nc.vector.tensor_copy(out=pages[t][:].indirect(half_offs[h]), in_=values)
+
+        for t in range(PACK):
+            nc.vector.tensor_copy(out=xg[:, t, :], in_=x_planes[t][:].indirect(offs_sb[:]))
+            nc.vector.tensor_copy(out=xe0[:, t, :], in_=xg[:, t, :].indirect(half_offs[0]))
+            if t % 2 == 1:
+                weave(nc.scalar.copy, xe0_woven, xe0[:, t - 1 : t + 1, :], t // 2, whole)
+
+        xe1_low = keep.tile([P, 2, HALF], F32, name="xe1_low", tag="x_plane3")
+        for e in range(2):
+            nc.vector.tensor_copy(out=xe1_low[:, e, :], in_=xg[:, e, :].indirect(half_offs[1]))
+        nc.vector.tensor_copy(
+            out=wa[:].bitcast(I32).rearrange("p (t m) -> p t m", t=PACK),
+            in_=wa_raw[:].bitcast(I32).rearrange("p (m t) -> p t m", t=PACK),
+        )
+        quantize(nc, xe0_codes, xe0_scales, xe0_woven, whole)
+        xe1_high = keep.tile([P, 2, HALF], F32, name="xe1_high", tag="hold_a", align_bytes=64)
+        for e in range(2):
+            nc.vector.tensor_copy(out=xe1_high[:, e, :], in_=xg[:, 2 + e, :].indirect(half_offs[1]))
+
+        q0 = keep.tile([P, PACK, HALF], F32, name="q0")
+        q1 = keep.tile([P, PACK, HALF], F32, name="q1")
+        acc0 = [psum.tile([P, 2, HALF], F32, name="acc0_%d" % u, tag="bank%d" % u) for u in range(2)]
+        for t in range(PACK):
+            expert(acc0[t // 2][:, t % 2, :], t, xe0_codes, xe0_scales)
+        nc.scalar.copy(out=q0[:, 0:2, :], in_=acc0[0][:])
+        for t in range(2):
+            scatter(t, 0, q0[:, t, :])
+
+        xe1_woven = keep.tile([P, HALF, PACK], BF16, name="xe1_woven", tag="hold_b", align_bytes=64)
+        weave(nc.scalar.copy, xe1_woven, xe1_low[:], 0, whole)
+        weave(nc.scalar.copy, xe1_woven, xe1_high[:], 1, whole)
+        quantize(nc, xe1_codes, xe1_scales, xe1_woven, whole)
+        nc.scalar.copy(out=q0[:, 2:4, :], in_=acc0[1][:])
+        for t in range(2, PACK):
+            scatter(t, 0, q0[:, t, :])
+
+        xg_woven = keep.tile([P, J, PACK], BF16, name="xg_woven", tag="hold_c", align_bytes=64)
+        for cols in chunks:
+            nc.scalar.copy(
+                out=xg_woven[:, cols, :].rearrange("p (c i) t -> p c t i", i=4),
+                in_=xg[:, :, cols].rearrange("p t (c i) -> p c t i", i=4),
+            )
+            quantize(nc, xg_codes, xg_scales, xg_woven, cols)
+
+        acc1 = psum.tile([P, 2, HALF], F32, name="acc1", tag="bank2")
+        for t in range(2):
+            expert(acc1[:, t, :], t, xe1_codes, xe1_scales)
+        nc.scalar.copy(out=q1[:, 0:2, :], in_=acc1[:])
+
+        p_banks = []
+        for t in range(PACK):
+            for b, cols in enumerate(banks):
+                acc = psum.tile([P, BANK], F32, name="p%d_%d" % (t, b), tag="bank%d" % ((3 + 2 * t + b) % 8))
+                nc.tensor.matmul_mx(
+                    out=acc[:],
+                    lhsT=wa[:, P * t : P * (t + 1)].bitcast(FP8X4),
+                    lhsT_scale=sc[:, P * t : P * (t + 1)],
+                    rhs=xg_codes[:, cols].bitcast(FP8X4),
+                    rhs_scale=xg_scales[:, cols],
+                    start=True,
+                    stop=True,
+                )
+                p_banks.append(acc)
+
+        y = keep.tile([P, PACK, J], F32, name="y")
+        y_woven = keep.tile([P, J, PACK], BF16, name="y_woven", align_bytes=64)
+        y_codes = keep.tile([P, J], U32, name="y_codes", align_bytes=64)
+        y_scales = keep.tile([P, J], U8, name="y_scales", align_bytes=64)
+        y_rows = out_0.rearrange("(p t) c -> t p c", t=PACK)
+        words_out = out_1[0].rearrange("p c t -> p (c t)").bitcast(I32)
+
+        def add(t, c0, width):
+            b, inside = divmod(c0, BANK)
+            nc.vector.tensor_tensor(
+                out=y[:, t, c0 : c0 + width],
+                in0=p_banks[2 * t + b][:, inside : inside + width],
+                in1=pages[t][:, c0 : c0 + width],
+                op=ADD,
+            )
+
+        def finish_plane(t):
+            for cols in banks:
+                add(t, cols.start, BANK)
+            nc.sync.dma_start(out=y_rows[t], in_=y[:, t, :])
+
+        def late_expert(t):
+            acc = psum.tile([P, HALF], F32, name="late%d" % t, tag="bank%d" % (3 + 2 * (t - 2)))
+            expert(acc[:], t, xe1_codes, xe1_scales)
+            nc.scalar.copy(out=q1[:, t, :], in_=acc[:])
+
+        scatter(0, 1, q1[:, 0, :])
+        scatter(1, 1, q1[:, 1, :])
+        finish_plane(0)
+        late_expert(2)
+        finish_plane(1)
+        late_expert(3)
+        for cols in banks:
+            weave(nc.scalar.copy, y_woven, y[:, 0:2, :], 0, cols)
+        scatter(2, 1, q1[:, 2, :])
+        finish_plane(2)
+        scatter(3, 1, q1[:, 3, :])
+
+        for cols in chunks:
+            add(3, cols.start, CHUNK)
+            if cols.stop % BANK == 0:
+                nc.sync.dma_start(out=y_rows[3][:, cols.stop - BANK : cols.stop], in_=y[:, 3, cols.stop - BANK : cols.stop])
+        for c, cols in enumerate(chunks):
+            weave(nc.vector.tensor_copy if c == len(chunks) - 1 else nc.scalar.copy, y_woven, y[:, 2:4, :], 1, cols)
+        for cols in chunks:
+            quantize(nc, y_codes, y_scales, y_woven, cols)
+            nc.sync.dma_start(out=words_out[:, cols], in_=y_codes[:, cols].bitcast(I32))
+        for q in range(4):
+            queue = nc.scalar if q % 2 else nc.sync
+            queue.dma_start(out=out_2[0, 4 * q : 4 * q + 4, :].bitcast(I32), in_=y_scales[32 * q : 32 * q + 4, :].bitcast(I32))

@@ -20,6 +20,7 @@ PACK = 4
 BANK = 512
 HALF = I // 2
 CHUNK = 256
+WA_PLANE = 4
 
 
 def weave(engine_copy, woven, planes, pair, cols):
@@ -51,43 +52,48 @@ def tile_list_two_level_routing_pl_kernel(tc, xf, wa_words, wa_scales, wb_words,
         x_planes = [keep.tile([P, T], F32, name="x_plane%d" % t, tag="x_plane%d" % t) for t in range(PACK)]
         wa_raw = keep.tile([P, N], U32, name="wa_raw", align_bytes=64)
         wb_raw = keep.tile([P, 2 * N], U8, name="wb_raw", align_bytes=64)
-        sc_raw = keep.tile([P, 2 * N], U8, name="sc_raw", align_bytes=64)
+        sc_raw = keep.tile([P, N], U8, name="sc_raw", align_bytes=64)
         wa = keep.tile([P, N], U32, name="wa", align_bytes=64)
         wb = keep.tile([P, 2 * N], U8, name="wb", align_bytes=64)
-        sc = keep.tile([P, 2 * N], U8, name="sc", align_bytes=64)
+        sc = keep.tile([P, N], U8, name="sc", align_bytes=64)
         pages = [keep.tile([P, J], F32, name="page%d" % t) for t in range(PACK)]
 
         nc.vector.memset(sc_raw[:].bitcast(I32), 0)
         nc.sync.dma_start(offs_sb[:], offs)
-        nc.sync.dma_start(out=wb_raw[:].bitcast(I32), in_=wb_words[0].bitcast(I32))
         nc.sync.dma_start(out=x_planes[0][:], in_=x_rows[0])
-        for w, w_scales in enumerate((wa_scales, wb_scales)):
-            for q in range(4):
-                nc.scalar.dma_start(
-                    out=sc_raw[32 * q : 32 * q + 4, w * N : (w + 1) * N].bitcast(I32),
-                    in_=w_scales[0, 4 * q : 4 * q + 4, :].bitcast(I32),
-                )
         nc.sync.dma_start(offs2_sb[:], offs2)
-        for t in range(1, PACK):
-            nc.sync.dma_start(out=x_planes[t][:], in_=x_rows[t])
+        nc.sync.dma_start(out=wb_raw[:].bitcast(I32), in_=wb_words[0].bitcast(I32))
+        nc.sync.dma_start(out=x_planes[1][:], in_=x_rows[1])
         nc.sync.dma_start(out=wa_raw[:].bitcast(I32), in_=wa_words[0].rearrange("p n t -> p (n t)").bitcast(I32))
+        for t in range(2, PACK):
+            nc.sync.dma_start(out=x_planes[t][:], in_=x_rows[t])
+        for first_row, w_scales in ((0, wb_scales), (WA_PLANE, wa_scales)):
+            for quad in range(4):
+                nc.sync.dma_start(
+                    out=sc_raw[32 * quad + first_row : 32 * quad + first_row + 4, :].bitcast(I32),
+                    in_=w_scales[0, 4 * quad : 4 * quad + 4, :].bitcast(I32),
+                )
 
         for t in range(PACK):
-            nc.vector.memset(pages[t][:].bitcast(I32), 0)
-        nc.vector.tensor_copy(
-            out=wb[:].bitcast(U16).rearrange("p (t m) -> p t m", t=PACK),
-            in_=wb_raw[:].bitcast(U16).rearrange("p (m t) -> p t m", t=PACK),
+            nc.gpsimd.memset(pages[t][:], 0.0)
+        nc.gpsimd.tensor_copy(
+            out=wb[:].rearrange("p (t m b) -> p t m b", t=PACK, b=2),
+            in_=wb_raw[:].rearrange("p (m t b) -> p t m b", t=PACK, b=2),
         )
-        nc.vector.tensor_copy(
-            out=sc[:].rearrange("p (w t m) -> p w t m", w=2, t=PACK),
-            in_=sc_raw[:].rearrange("p (w m t) -> p w t m", w=2, t=PACK),
+        nc.gpsimd.tensor_copy(
+            out=wa[:].bitcast(I32).rearrange("p (t m) -> p t m", t=PACK),
+            in_=wa_raw[:].bitcast(I32).rearrange("p (m t) -> p t m", t=PACK),
+        )
+        nc.gpsimd.tensor_copy(
+            out=sc[:].rearrange("p (t m) -> p t m", t=PACK),
+            in_=sc_raw[:].rearrange("p (m t) -> p t m", t=PACK),
         )
 
         xg = keep.tile([P, PACK, J], F32, name="xg")
         xe0 = keep.tile([P, PACK, HALF], F32, name="xe0")
         xe0_woven = keep.tile([P, HALF, PACK], BF16, name="xe0_woven", tag="hold_a", align_bytes=64)
         xe0_codes = keep.tile([P, HALF], U32, name="xe0_codes", tag="hold_b", align_bytes=64)
-        xe0_scales = keep.tile([P, HALF], U8, name="xe0_scales", tag="hold_c", align_bytes=64)
+        xe0_scales = keep.tile([P, HALF], U8, name="xe0_scales", align_bytes=64)
         xe1_codes = keep.tile([P, HALF], U32, name="xe1_codes", align_bytes=64)
         xe1_scales = keep.tile([P, HALF], U8, name="xe1_scales", align_bytes=64)
         xg_codes = keep.tile([P, J], U32, name="xg_codes", align_bytes=64)
@@ -101,78 +107,89 @@ def tile_list_two_level_routing_pl_kernel(tc, xf, wa_words, wa_scales, wb_words,
             nc.tensor.matmul_mx(
                 out=acc,
                 lhsT=wb[:, 2 * P * t : 2 * P * (t + 1)].bitcast(FP4X4),
-                lhsT_scale=sc[:, N + P * t : N + P * (t + 1)],
+                lhsT_scale=sc[:, P * t : P * (t + 1)],
                 rhs=codes[:].bitcast(FP8X4),
                 rhs_scale=scales[:],
                 start=True,
                 stop=True,
             )
 
-        def scatter(t, h, values):
-            nc.vector.tensor_copy(out=pages[t][:].indirect(half_offs[h]), in_=values)
+        q = keep.tile([P, PACK, I], F32, name="q")
+        halves = [slice(h * HALF, (h + 1) * HALF) for h in range(2)]
 
+        def scatter(t, h):
+            nc.vector.tensor_copy(out=pages[t][:].indirect(half_offs[h]), in_=q[:, t, halves[h]])
+
+        xg_woven = keep.tile([P, J, PACK], BF16, name="xg_woven", align_bytes=64)
         for t in range(PACK):
             nc.vector.tensor_copy(out=xg[:, t, :], in_=x_planes[t][:].indirect(offs_sb[:]))
             nc.vector.tensor_copy(out=xe0[:, t, :], in_=xg[:, t, :].indirect(half_offs[0]))
             if t % 2 == 1:
                 weave(nc.scalar.copy, xe0_woven, xe0[:, t - 1 : t + 1, :], t // 2, whole)
+            if t == 1:
+                for cols in banks:
+                    weave(nc.scalar.copy, xg_woven, xg[:, 0:2, :], 0, cols)
 
         xe1_low = keep.tile([P, 2, HALF], F32, name="xe1_low", tag="x_plane3")
         for e in range(2):
             nc.vector.tensor_copy(out=xe1_low[:, e, :], in_=xg[:, e, :].indirect(half_offs[1]))
-        nc.vector.tensor_copy(
-            out=wa[:].bitcast(I32).rearrange("p (t m) -> p t m", t=PACK),
-            in_=wa_raw[:].bitcast(I32).rearrange("p (m t) -> p t m", t=PACK),
-        )
         quantize(nc, xe0_codes, xe0_scales, xe0_woven, whole)
         xe1_high = keep.tile([P, 2, HALF], F32, name="xe1_high", tag="hold_a", align_bytes=64)
         for e in range(2):
             nc.vector.tensor_copy(out=xe1_high[:, e, :], in_=xg[:, 2 + e, :].indirect(half_offs[1]))
 
-        q0 = keep.tile([P, PACK, HALF], F32, name="q0")
-        q1 = keep.tile([P, PACK, HALF], F32, name="q1")
-        acc0 = [psum.tile([P, 2, HALF], F32, name="acc0_%d" % u, tag="bank%d" % u) for u in range(2)]
-        for t in range(PACK):
-            expert(acc0[t // 2][:, t % 2, :], t, xe0_codes, xe0_scales)
-        nc.scalar.copy(out=q0[:, 0:2, :], in_=acc0[0][:])
-        for t in range(2):
-            scatter(t, 0, q0[:, t, :])
+        early = [psum.tile([P, HALF], F32, name="early%d" % t, tag="bank%d" % t) for t in range(2)]
+        both = [psum.tile([P, I], F32, name="both%d" % t, tag="bank%d" % t) for t in range(2, PACK)]
+        expert(early[0][:], 0, xe0_codes, xe0_scales)
+        for t in range(2, PACK):
+            expert(both[t - 2][:, halves[0]], t, xe0_codes, xe0_scales)
+        expert(early[1][:], 1, xe0_codes, xe0_scales)
+        nc.scalar.copy(out=q[:, 0, halves[0]], in_=early[0][:])
+        scatter(0, 0)
 
         xe1_woven = keep.tile([P, HALF, PACK], BF16, name="xe1_woven", tag="hold_b", align_bytes=64)
         weave(nc.scalar.copy, xe1_woven, xe1_low[:], 0, whole)
         weave(nc.scalar.copy, xe1_woven, xe1_high[:], 1, whole)
         quantize(nc, xe1_codes, xe1_scales, xe1_woven, whole)
-        nc.scalar.copy(out=q0[:, 2:4, :], in_=acc0[1][:])
-        for t in range(2, PACK):
-            scatter(t, 0, q0[:, t, :])
+        nc.scalar.copy(out=q[:, 1, halves[0]], in_=early[1][:])
+        scatter(1, 0)
 
-        xg_woven = keep.tile([P, J, PACK], BF16, name="xg_woven", tag="hold_c", align_bytes=64)
+        late = psum.tile([P, 2, HALF], F32, name="late", tag="bank0")
+        for t in range(2):
+            expert(late[:, t, :], t, xe1_codes, xe1_scales)
+        for t in range(2, PACK):
+            expert(both[t - 2][:, halves[1]], t, xe1_codes, xe1_scales)
+        nc.scalar.copy(out=q[:, 0:2, halves[1]], in_=late[:])
+
         for cols in chunks:
-            nc.scalar.copy(
-                out=xg_woven[:, cols, :].rearrange("p (c i) t -> p c t i", i=4),
-                in_=xg[:, :, cols].rearrange("p t (c i) -> p c t i", i=4),
-            )
+            weave(nc.scalar.copy, xg_woven, xg[:, 2:4, :], 1, cols)
             quantize(nc, xg_codes, xg_scales, xg_woven, cols)
 
-        acc1 = psum.tile([P, 2, HALF], F32, name="acc1", tag="bank2")
-        for t in range(2):
-            expert(acc1[:, t, :], t, xe1_codes, xe1_scales)
-        nc.scalar.copy(out=q1[:, 0:2, :], in_=acc1[:])
+        p_banks = {}
+        p_sb = keep.tile([P, PACK - 1, J], F32, name="p_sb")
 
-        p_banks = []
-        for t in range(PACK):
+        def group_product(t):
             for b, cols in enumerate(banks):
-                acc = psum.tile([P, BANK], F32, name="p%d_%d" % (t, b), tag="bank%d" % ((3 + 2 * t + b) % 8))
+                acc = psum.tile([P, BANK], F32, name="p%d_%d" % (t, b), tag="bank%d" % (4, 5, 6, 7, 1, 0, 2, 3)[2 * t + b])
                 nc.tensor.matmul_mx(
                     out=acc[:],
                     lhsT=wa[:, P * t : P * (t + 1)].bitcast(FP8X4),
-                    lhsT_scale=sc[:, P * t : P * (t + 1)],
+                    lhsT_scale=sc[WA_PLANE:, P * t : P * (t + 1)],
                     rhs=xg_codes[:, cols].bitcast(FP8X4),
                     rhs_scale=xg_scales[:, cols],
                     start=True,
                     stop=True,
                 )
-                p_banks.append(acc)
+                p_banks[2 * t + b] = acc
+                if t < PACK - 1:
+                    nc.scalar.copy(out=p_sb[:, t, cols], in_=acc[:])
+
+        group_product(0)
+        nc.scalar.copy(out=q[:, 2, :], in_=both[0][:])
+        group_product(1)
+        nc.scalar.copy(out=q[:, 3, :], in_=both[1][:])
+        group_product(2)
+        group_product(3)
 
         y = keep.tile([P, PACK, J], F32, name="y")
         y_woven = keep.tile([P, J, PACK], BF16, name="y_woven", align_bytes=64)
@@ -190,27 +207,16 @@ def tile_list_two_level_routing_pl_kernel(tc, xf, wa_words, wa_scales, wb_words,
                 op=ADD,
             )
 
-        def finish_plane(t):
+        scatter(0, 1)
+        scatter(1, 1)
+        for t in range(2, PACK):
+            nc.vector.tensor_copy(out=pages[t][:].indirect(offs2_sb[:]), in_=q[:, t, :])
+        for t in range(PACK - 1):
             for cols in banks:
-                add(t, cols.start, BANK)
-            nc.sync.dma_start(out=y_rows[t], in_=y[:, t, :])
-
-        def late_expert(t):
-            acc = psum.tile([P, HALF], F32, name="late%d" % t, tag="bank%d" % (3 + 2 * (t - 2)))
-            expert(acc[:], t, xe1_codes, xe1_scales)
-            nc.scalar.copy(out=q1[:, t, :], in_=acc[:])
-
-        scatter(0, 1, q1[:, 0, :])
-        scatter(1, 1, q1[:, 1, :])
-        finish_plane(0)
-        late_expert(2)
-        finish_plane(1)
-        late_expert(3)
-        for cols in banks:
-            weave(nc.scalar.copy, y_woven, y[:, 0:2, :], 0, cols)
-        scatter(2, 1, q1[:, 2, :])
-        finish_plane(2)
-        scatter(3, 1, q1[:, 3, :])
+                nc.gpsimd.tensor_tensor(out=y[:, t, cols], in0=p_sb[:, t, cols], in1=pages[t][:, cols], op=ADD)
+                if t == 1:
+                    weave(nc.scalar.copy, y_woven, y[:, 0:2, :], 0, cols)
+            nc.scalar.dma_start(out=y_rows[t], in_=y[:, t, :])
 
         for cols in chunks:
             add(3, cols.start, CHUNK)
@@ -221,6 +227,6 @@ def tile_list_two_level_routing_pl_kernel(tc, xf, wa_words, wa_scales, wb_words,
         for cols in chunks:
             quantize(nc, y_codes, y_scales, y_woven, cols)
             nc.sync.dma_start(out=words_out[:, cols], in_=y_codes[:, cols].bitcast(I32))
-        for q in range(4):
-            queue = nc.scalar if q % 2 else nc.sync
-            queue.dma_start(out=out_2[0, 4 * q : 4 * q + 4, :].bitcast(I32), in_=y_scales[32 * q : 32 * q + 4, :].bitcast(I32))
+        for quad in range(4):
+            queue = nc.scalar if quad % 2 else nc.sync
+            queue.dma_start(out=out_2[0, 4 * quad : 4 * quad + 4, :].bitcast(I32), in_=y_scales[32 * quad : 32 * quad + 4, :].bitcast(I32))

from contextlib import ExitStack

import concourse.mybir as mybir

K, T, J, I, N = 512, 2048, 1024, 512, 512
FLOPS = 2 * K * N * (J + I)

F32 = mybir.dt.float32
BF16 = mybir.dt.bfloat16
I32 = mybir.dt.int32
U32 = mybir.dt.uint32
U16 = mybir.dt.uint16
U8 = mybir.dt.uint8
FP8X4 = mybir.dt.float8_e4m3fn_x4
FP4X4 = mybir.dt.float4_e2m1fn_x4
ADD = mybir.AluOpType.add

P = 128
PACK = 4
BANK = 512
HALF = I // 2
CHUNK = 256
WA_PLANE = 4


def weave(engine_copy, woven, planes, pair, cols):
    engine_copy(
        out=woven[:, cols, 2 * pair : 2 * pair + 2],
        in_=planes[:, :, cols].rearrange("p t c -> p c t"),
    )


def quantize(nc, codes, scales, woven, cols):
    nc.vector.quantize_mx(
        out=codes[:, cols].bitcast(FP8X4),
        scales=scales[:, cols],
        in_=woven[:, cols, :].rearrange("p c t -> p (c t)"),
    )


def tile_list_two_level_routing_pl_kernel(tc, xf, wa_words, wa_scales, wb_words, wb_scales, offs, offs2, out_0, out_1, out_2):
    nc = tc.nc
    with ExitStack() as ctx:
        lists = ctx.enter_context(tc.tile_pool(name="lists", bufs=1))
        keep = ctx.enter_context(tc.tile_pool(name="keep", bufs=1))
        psum = ctx.enter_context(tc.psum_pool(name="psum", bufs=1))

        offs_sb = lists.tile([P, J // 16], U16, name="offs_sb")
        offs2_sb = lists.tile([P, I // 16], U16, name="offs2_sb")

        x_rows = xf.rearrange("(p t) c -> t p c", t=PACK)
        x_planes = [keep.tile([P, T], F32, name="x_plane%d" % t, tag="x_plane%d" % t) for t in range(PACK)]
        wa_raw = keep.tile([P, N], U32, name="wa_raw", align_bytes=64)
        wb_raw = keep.tile([P, 2 * N], U8, name="wb_raw", align_bytes=64)
        sc_raw = keep.tile([P, N], U8, name="sc_raw", align_bytes=64)
        wa = keep.tile([P, N], U32, name="wa", align_bytes=64)
        wb = keep.tile([P, 2 * N], U8, name="wb", align_bytes=64)
        sc = keep.tile([P, N], U8, name="sc", align_bytes=64)
        pages = [keep.tile([P, J], F32, name="page%d" % t) for t in range(PACK)]

        nc.vector.memset(sc_raw[:].bitcast(I32), 0)
        nc.sync.dma_start(offs_sb[:], offs)
        nc.sync.dma_start(out=x_planes[0][:], in_=x_rows[0])
        nc.sync.dma_start(offs2_sb[:], offs2)
        nc.sync.dma_start(out=wb_raw[:].bitcast(I32), in_=wb_words[0].bitcast(I32))
        nc.sync.dma_start(out=x_planes[1][:], in_=x_rows[1])
        nc.sync.dma_start(out=wa_raw[:].bitcast(I32), in_=wa_words[0].rearrange("p n t -> p (n t)").bitcast(I32))
        for t in range(2, PACK):
            nc.sync.dma_start(out=x_planes[t][:], in_=x_rows[t])
        for first_row, w_scales in ((0, wb_scales), (WA_PLANE, wa_scales)):
            for quad in range(4):
                nc.sync.dma_start(
                    out=sc_raw[32 * quad + first_row : 32 * quad + first_row + 4, :].bitcast(I32),
                    in_=w_scales[0, 4 * quad : 4 * quad + 4, :].bitcast(I32),
                )

        for t in range(PACK):
            nc.gpsimd.memset(pages[t][:], 0.0)
        nc.gpsimd.tensor_copy(
            out=wb[:].rearrange("p (t m b) -> p t m b", t=PACK, b=2),
            in_=wb_raw[:].rearrange("p (m t b) -> p t m b", t=PACK, b=2),
        )
        nc.gpsimd.tensor_copy(
            out=wa[:].bitcast(I32).rearrange("p (t m) -> p t m", t=PACK),
            in_=wa_raw[:].bitcast(I32).rearrange("p (m t) -> p t m", t=PACK),
        )
        nc.gpsimd.tensor_copy(
            out=sc[:].rearrange("p (t m) -> p t m", t=PACK),
            in_=sc_raw[:].rearrange("p (m t) -> p t m", t=PACK),
        )

        xg = keep.tile([P, PACK, J], F32, name="xg")
        xe0 = keep.tile([P, PACK, HALF], F32, name="xe0")
        xe0_woven = keep.tile([P, HALF, PACK], BF16, name="xe0_woven", tag="hold_a", align_bytes=64)
        xe0_codes = keep.tile([P, HALF], U32, name="xe0_codes", tag="hold_b", align_bytes=64)
        xe0_scales = keep.tile([P, HALF], U8, name="xe0_scales", align_bytes=64)
        xe1_codes = keep.tile([P, HALF], U32, name="xe1_codes", align_bytes=64)
        xe1_scales = keep.tile([P, HALF], U8, name="xe1_scales", align_bytes=64)
        xg_codes = keep.tile([P, J], U32, name="xg_codes", align_bytes=64)
        xg_scales = keep.tile([P, J], U8, name="xg_scales", align_bytes=64)
        half_offs = [offs2_sb[:, h * (HALF // 16) : (h + 1) * (HALF // 16)] for h in range(2)]
        whole = slice(0, HALF)
        banks = [slice(b * BANK, (b + 1) * BANK) for b in range(J // BANK)]
        chunks = [slice(c, c + CHUNK) for c in range(0, J, CHUNK)]

        def expert(acc, t, codes, scales):
            nc.tensor.matmul_mx(
                out=acc,
                lhsT=wb[:, 2 * P * t : 2 * P * (t + 1)].bitcast(FP4X4),
                lhsT_scale=sc[:, P * t : P * (t + 1)],
                rhs=codes[:].bitcast(FP8X4),
                rhs_scale=scales[:],
                start=True,
                stop=True,
            )

        q = keep.tile([P, PACK, I], F32, name="q")
        halves = [slice(h * HALF, (h + 1) * HALF) for h in range(2)]

        def scatter(t, h):
            nc.vector.tensor_copy(out=pages[t][:].indirect(half_offs[h]), in_=q[:, t, halves[h]])

        xg_woven = keep.tile([P, J, PACK], BF16, name="xg_woven", align_bytes=64)
        for t in range(PACK):
            nc.vector.tensor_copy(out=xg[:, t, :], in_=x_planes[t][:].indirect(offs_sb[:]))
            nc.vector.tensor_copy(out=xe0[:, t, :], in_=xg[:, t, :].indirect(half_offs[0]))
            if t % 2 == 1:
                weave(nc.scalar.copy, xe0_woven, xe0[:, t - 1 : t + 1, :], t // 2, whole)
            if t == 1:
                for cols in banks:
                    weave(nc.scalar.copy, xg_woven, xg[:, 0:2, :], 0, cols)

        xe1_low = keep.tile([P, 2, HALF], F32, name="xe1_low", tag="x_plane3")
        for e in range(2):
            nc.vector.tensor_copy(out=xe1_low[:, e, :], in_=xg[:, e, :].indirect(half_offs[1]))
        quantize(nc, xe0_codes, xe0_scales, xe0_woven, whole)
        xe1_high = keep.tile([P, 2, HALF], F32, name="xe1_high", tag="hold_a", align_bytes=64)
        for e in range(2):
            nc.vector.tensor_copy(out=xe1_high[:, e, :], in_=xg[:, 2 + e, :].indirect(half_offs[1]))

        early = [psum.tile([P, HALF], F32, name="early%d" % t, tag="bank%d" % t) for t in range(2)]
        both = [psum.tile([P, I], F32, name="both%d" % t, tag="bank%d" % t) for t in range(2, PACK)]
        expert(early[0][:], 0, xe0_codes, xe0_scales)
        for t in range(2, PACK):
            expert(both[t - 2][:, halves[0]], t, xe0_codes, xe0_scales)
        expert(early[1][:], 1, xe0_codes, xe0_scales)
        nc.scalar.copy(out=q[:, 0, halves[0]], in_=early[0][:])
        scatter(0, 0)

        xe1_woven = keep.tile([P, HALF, PACK], BF16, name="xe1_woven", tag="hold_b", align_bytes=64)
        weave(nc.scalar.copy, xe1_woven, xe1_low[:], 0, whole)
        weave(nc.scalar.copy, xe1_woven, xe1_high[:], 1, whole)
        quantize(nc, xe1_codes, xe1_scales, xe1_woven, whole)
        nc.scalar.copy(out=q[:, 1, halves[0]], in_=early[1][:])
        scatter(1, 0)

        late = psum.tile([P, 2, HALF], F32, name="late", tag="bank0")
        for t in range(2):
            expert(late[:, t, :], t, xe1_codes, xe1_scales)
        for t in range(2, PACK):
            expert(both[t - 2][:, halves[1]], t, xe1_codes, xe1_scales)
        nc.scalar.copy(out=q[:, 0:2, halves[1]], in_=late[:])

        for cols in chunks:
            weave(nc.scalar.copy, xg_woven, xg[:, 2:4, :], 1, cols)
            quantize(nc, xg_codes, xg_scales, xg_woven, cols)

        p_banks = {}
        p_sb = keep.tile([P, PACK - 1, J], F32, name="p_sb")

        def group_product(t):
            for b, cols in enumerate(banks):
                acc = psum.tile([P, BANK], F32, name="p%d_%d" % (t, b), tag="bank%d" % (4, 5, 6, 7, 1, 0, 2, 3)[2 * t + b])
                nc.tensor.matmul_mx(
                    out=acc[:],
                    lhsT=wa[:, P * t : P * (t + 1)].bitcast(FP8X4),
                    lhsT_scale=sc[WA_PLANE:, P * t : P * (t + 1)],
                    rhs=xg_codes[:, cols].bitcast(FP8X4),
                    rhs_scale=xg_scales[:, cols],
                    start=True,
                    stop=True,
                )
                p_banks[2 * t + b] = acc
                if t < PACK - 1:
                    nc.scalar.copy(out=p_sb[:, t, cols], in_=acc[:])

        group_product(0)
        nc.scalar.copy(out=q[:, 2, :], in_=both[0][:])
        group_product(1)
        nc.scalar.copy(out=q[:, 3, :], in_=both[1][:])
        group_product(2)
        group_product(3)

        y = keep.tile([P, PACK, J], F32, name="y")
        y_woven = keep.tile([P, J, PACK], BF16, name="y_woven", align_bytes=64)
        y_codes = keep.tile([P, J], U32, name="y_codes", align_bytes=64)
        y_scales = keep.tile([P, J], U8, name="y_scales", align_bytes=64)
        y_rows = out_0.rearrange("(p t) c -> t p c", t=PACK)
        words_out = out_1[0].rearrange("p c t -> p (c t)").bitcast(I32)

        def add(t, c0, width):
            b, inside = divmod(c0, BANK)
            nc.vector.tensor_tensor(
                out=y[:, t, c0 : c0 + width],
                in0=p_banks[2 * t + b][:, inside : inside + width],
                in1=pages[t][:, c0 : c0 + width],
                op=ADD,
            )

        scatter(0, 1)
        scatter(1, 1)
        for t in range(2, PACK):
            nc.vector.tensor_copy(out=pages[t][:].indirect(offs2_sb[:]), in_=q[:, t, :])
        for t in range(PACK - 1):
            for cols in banks:
                nc.gpsimd.tensor_tensor(out=y[:, t, cols], in0=p_sb[:, t, cols], in1=pages[t][:, cols], op=ADD)
                if t == 1:
                    weave(nc.scalar.copy, y_woven, y[:, 0:2, :], 0, cols)
            nc.scalar.dma_start(out=y_rows[t], in_=y[:, t, :])

        for cols in chunks:
            add(3, cols.start, CHUNK)
            if cols.stop % BANK == 0:
                nc.sync.dma_start(out=y_rows[3][:, cols.stop - BANK : cols.stop], in_=y[:, 3, cols.stop - BANK : cols.stop])
        for c, cols in enumerate(chunks):
            weave(nc.vector.tensor_copy if c == len(chunks) - 1 else nc.scalar.copy, y_woven, y[:, 2:4, :], 1, cols)
        for cols in chunks:
            quantize(nc, y_codes, y_scales, y_woven, cols)
            nc.sync.dma_start(out=words_out[:, cols], in_=y_codes[:, cols].bitcast(I32))
        for quad in range(4):
            queue = nc.scalar if quad % 2 else nc.sync
            queue.dma_start(out=out_2[0, 4 * quad : 4 * quad + 4, :].bitcast(I32), in_=y_scales[32 * quad : 32 * quad + 4, :].bitcast(I32))
